import numpy as np
import ml_dtypes


def mxq(x, axis, fmt="e4m3"):
    dtype, down = {"e4m3": (ml_dtypes.float8_e4m3fn, 7), "e5m2": (ml_dtypes.float8_e5m2, 14)}[fmt]
    v = np.moveaxis(np.asarray(x, np.float32).astype(ml_dtypes.bfloat16).astype(np.float64), axis, -1)
    blocks = v.reshape(v.shape[:-1] + (-1, 32))
    amax = np.abs(blocks).max(-1, keepdims=True)
    byte = np.maximum(np.where(amax > 0, np.frexp(amax)[1] - 1 + 127, 0) - down, 1)
    scale = np.exp2(byte - 127.0)
    codes = (blocks / scale).astype(np.float32).astype(dtype).astype(np.float64)
    return np.moveaxis((codes * scale).reshape(v.shape), -1, axis)


WIDE = False


def mx_kscale(k):
    if not WIDE:
        return np.ones(k)
    levels = np.array([30, -30])
    if k % 512:
        return np.exp2(np.random.permutation(np.resize(levels, k // 32))).repeat(32)
    a = np.empty((k // 512, 16))
    for p in range(k // 512):
        a[p, :8] = np.random.permutation(np.resize(levels, 8))
        for g in range(8):
            far = levels[np.abs(levels - a[p, g]) >= 10]
            a[p, g + 8] = far[np.random.randint(len(far))]
    return np.exp2(a.ravel()).repeat(32)


def f64(x):
    return np.asarray(x).astype(np.float64)


def striped(idx):
    return np.tile(np.asarray(idx).reshape(-1, 16).T, (8, 1)).astype(np.uint16)


def unstriped(offs):
    return offs[:16].T.reshape(-1).astype(np.int64)


E2M1 = np.array([0.0, 0.5, 1.0, 1.5, 2.0, 3.0, 4.0, 6.0, -0.0, -0.5, -1.0, -1.5, -2.0, -3.0, -4.0, -6.0])


def pack_weight(w, fmt):
    k, n = w.shape
    w = f64(np.asarray(w, np.float32).astype(ml_dtypes.bfloat16)).reshape(k // 32, 32, n)
    amax = np.abs(w).max(1)
    if fmt in ("e4m3", "e5m2"):
        byte = np.frexp(amax)[1] - 1 + 127 - (7 if fmt == "e4m3" else 14)
    else:
        mant, ex = np.frexp(amax / 6.0)
        byte = np.where(mant > 0.5, ex, ex - 1) + 127
    byte = np.clip(np.where(amax > 0, byte, 1), 1, 254)
    scaled = (w * np.exp2(127.0 - byte)[:, None, :]).reshape(k, n).astype(np.float32)
    by_word = np.ascontiguousarray(scaled.reshape(k // 512, 128, 4, n).transpose(0, 1, 3, 2))
    if fmt in ("e4m3", "e5m2"):
        words = by_word.astype(ml_dtypes.float8_e4m3fn if fmt == "e4m3" else ml_dtypes.float8_e5m2).view(np.uint8)
    else:
        c = by_word.astype(ml_dtypes.float4_e2m1fn).view(np.uint8) & 0xF
        words = (c[..., 0::2] | (c[..., 1::2] << 4)).reshape(k // 512, 128, 2 * n)
    return np.ascontiguousarray(words), np.ascontiguousarray(byte.astype(np.uint8).reshape(k // 512, 16, n))


def unpack_weight(words, scales, fmt):
    g, _, n = scales.shape
    words = np.ascontiguousarray(words).reshape(g, 128, n, -1)
    if fmt in ("e4m3", "e5m2"):
        vals = words.view(ml_dtypes.float8_e4m3fn if fmt == "e4m3" else ml_dtypes.float8_e5m2).astype(np.float64)
    else:
        nib = np.empty((g, 128, n, 4), np.uint8)
        nib[..., 0::2] = words & 0xF
        nib[..., 1::2] = words >> 4
        vals = E2M1[nib]
    vals = vals * np.repeat(np.exp2(scales.astype(np.float64) - 127.0), 8, axis=1)[..., None]
    return vals.transpose(0, 1, 3, 2).reshape(g * 512, n)


K, T, J, R, V, N, Z = 1024, 1024, 384, 512, 512, 256, 512


def setup_inputs():
    n = np.random.standard_normal
    idx = np.random.permutation(T)[:J]
    idx2 = np.random.permutation(V)[:J]
    idx3 = np.random.permutation(Z)[:J]
    fk = mx_kscale(K)
    fr = mx_kscale(R)
    xtp = pack_weight(n((K, T)) / fk[:, None], "e4m3")
    wp = pack_weight(n((K, R)) * 1 / np.sqrt(K) * fk[:, None] * fr, "e2m1")
    wbp = pack_weight(n((R, N)) * 1 / np.sqrt(R) / fr[:, None], "e5m2")
    return {
        "xt_words": xtp[0],
        "xt_scales": xtp[1],
        "w_words": wp[0],
        "w_scales": wp[1],
        "tb": (n((R, V)) * 0.7 * fr[:, None]).astype(np.float32),
        "wb_words": wbp[0],
        "wb_scales": wbp[1],
        "tz": (n((N, Z)) * 0.6).astype(np.float32),
        "rw": (np.random.uniform(0.5, 2.0, (1, J))).astype(np.float32),
        "offs": striped(idx),
        "offs2": striped(idx2),
        "offs3": striped(idx3),
    }


def reference(xt_words, xt_scales, w_words, w_scales, tb, wb_words, wb_scales, tz, rw, offs, offs2, offs3):
    idx = unstriped(offs)
    idx2 = unstriped(offs2)
    idx3 = unstriped(offs3)
    xtu = unpack_weight(xt_words, xt_scales, "e4m3")
    wu = unpack_weight(w_words, w_scales, "e2m1")
    wbu = unpack_weight(wb_words, wb_scales, "e5m2")
    xtidxg = xtu[:, idx]
    a = wu.T @ xtidxg
    hid = np.maximum(a, f64(tb)[:, idx2])
    hidq = mxq(hid, 0, "e4m3")
    p = wbu.T @ hidq
    y = np.maximum(p, f64(tz)[:, idx3]) * f64(rw)
    return y

@@ -1,0 +1,201 @@
+from contextlib import ExitStack
+
+import concourse.mybir as mybir
+from concourse.masks import make_identity
+
+K, T, J, R, V, N, Z = 1024, 1024, 384, 512, 512, 256, 512
+FLOPS = 2 * K * R * J + 2 * R * N * J
+
+F32 = mybir.dt.float32
+BF16 = mybir.dt.bfloat16
+I32 = mybir.dt.int32
+U32 = mybir.dt.uint32
+U16 = mybir.dt.uint16
+U8 = mybir.dt.uint8
+E4M3X4 = mybir.dt.float8_e4m3fn_x4
+E5M2X4 = mybir.dt.float8_e5m2_x4
+E2M1X4 = mybir.dt.float4_e2m1fn_x4
+MAX = mybir.AluOpType.max
+MULT = mybir.AluOpType.mult
+COPY = mybir.ActivationFunctionType.Copy
+
+P = 128
+PACK = 4
+PASSES = K // (P * PACK)
+CHUNK = 128
+CHUNKS = J // CHUNK
+HALVES = N // P
+LIST_COLS = CHUNK // 16
+
+
+def load_scale_rows(queue, plane, scales):
+    words = scales.bitcast(I32)
+    for q in range(4):
+        queue.dma_start(
+            out=plane[32 * q : 32 * q + 4, :, :],
+            in_=words[:, 4 * q : 4 * q + 4, :].rearrange("z r c -> r z c"),
+        )
+
+
+def tile_list_picked_abovetable_floored_kernel(
+    tc, xt_words, xt_scales, w_words, w_scales, tb, wb_words, wb_scales, tz, rw, offs, offs2, offs3, out
+):
+    nc = tc.nc
+    with ExitStack() as ctx:
+        sb = ctx.enter_context(tc.tile_pool(name="sb", bufs=1))
+        ps = ctx.enter_context(tc.psum_pool(name="ps", bufs=1))
+
+        idx = sb.tile([P, J // 16], U16, name="idx")
+        idx2 = sb.tile([P, J // 16], U16, name="idx2")
+        idx3 = sb.tile([P, J // 16], U16, name="idx3")
+        xs = sb.tile([P, PASSES, T // 4], I32, name="xs", align_bytes=64)
+        ws_raw = sb.tile([P, PASSES, R // 4], I32, name="ws_raw", align_bytes=64)
+        wbs = sb.tile([P, 1, N // 4], I32, name="wbs", align_bytes=64)
+        xw = [sb.tile([P, T], I32, name=f"xw{z}", align_bytes=64) for z in range(PASSES)]
+        w_raw = sb.tile([P, PASSES, R // 2], I32, name="w_raw", align_bytes=64)
+        tb_groups = [(0, 2), (2, 3), (3, 4)]
+        tbt = [sb.tile([P, t1 - t0, V], F32, name=f"tbt{t0}", align_bytes=64) for t0, t1 in tb_groups]
+        tzt = sb.tile([P, HALVES, Z], F32, name="tzt", align_bytes=64)
+        wbw = sb.tile([P, N], I32, name="wbw", align_bytes=64)
+        rwc = sb.tile([P, CHUNKS], F32, name="rwc", align_bytes=64)
+        ident = sb.tile([P, P], F32, name="ident", align_bytes=64)
+
+        nc.vector.memset(xs[:], 0)
+        nc.vector.memset(ws_raw[:], 0)
+        nc.gpsimd.memset(wbs[:], 0)
+
+        tb_rows = tb.rearrange("(p t) v -> p t v", t=PACK)
+        nc.sync.dma_start(idx[:], offs)
+        nc.sync.dma_start(out=w_raw[:], in_=w_words.bitcast(I32).rearrange("z p c -> p z c"))
+        load_scale_rows(nc.sync, xs, xt_scales)
+        nc.sync.dma_start(idx2[:], offs2)
+        nc.sync.dma_start(out=tbt[0][:], in_=tb_rows[:, 0:2, :])
+        nc.sync.dma_start(out=xw[0][:], in_=xt_words[0].rearrange("p c r -> p (c r)").bitcast(I32))
+        load_scale_rows(nc.sync, ws_raw, w_scales)
+        nc.sync.dma_start(out=tbt[1][:], in_=tb_rows[:, 2:3, :])
+        nc.sync.dma_start(out=xw[1][:], in_=xt_words[1].rearrange("p c r -> p (c r)").bitcast(I32))
+        nc.sync.dma_start(out=tbt[2][:], in_=tb_rows[:, 3:4, :])
+        nc.sync.dma_start(out=tzt[:], in_=tz.rearrange("(h p) z -> p h z", p=P))
+        nc.sync.dma_start(idx3[:], offs3)
+        nc.sync.dma_start(out=wbw[:], in_=wb_words[0].rearrange("p c r -> p (c r)").bitcast(I32))
+        load_scale_rows(nc.sync, wbs, wb_scales)
+        make_identity(nc, ident[:])
+        with nc.allow_non_contiguous_dma(reason="one weight to a partition"):
+            nc.gpsimd.dma_start(out=rwc[:], in_=rw.rearrange("o (c p) -> p (o c)", p=P))
+
+        xs_bytes = xs[:].bitcast(U8)
+        gs = [sb.tile([P, J], U8, name=f"gs{z}", align_bytes=64) for z in range(PASSES)]
+        gw = [sb.tile([P, J], U32, name=f"gw{z}", align_bytes=64) for z in range(PASSES)]
+        wp = sb.tile([P, PASSES, 2 * R], U8, name="wp", align_bytes=64)
+        wsp = sb.tile([P, PASSES, R], U8, name="wsp", align_bytes=64)
+        for z in range(PASSES):
+            nc.vector.tensor_copy(gs[z][:], xs_bytes[:, z, :].indirect(idx[:]))
+        for z in range(PASSES):
+            nc.vector.tensor_copy(
+                out=wsp[:, z, :].rearrange("p (t m) -> p t m", t=PACK),
+                in_=ws_raw[:, z, :].bitcast(U8).rearrange("p (m t) -> p t m", t=PACK),
+            )
+        for a in range(CHUNKS):
+            for z in range(PASSES):
+                nc.vector.tensor_copy(
+                    gw[z][:, a * CHUNK : (a + 1) * CHUNK],
+                    xw[z][:].bitcast(U32).indirect(idx[:, a * LIST_COLS : (a + 1) * LIST_COLS]),
+                )
+
+        tg = [sb.tile([P, PACK, CHUNK], F32, name=f"tg{a}", align_bytes=64) for a in range(CHUNKS)]
+        zg = [sb.tile([P, HALVES, CHUNK], F32, name=f"zg{a}", align_bytes=64) for a in range(CHUNKS)]
+
+        def gather_tb(a):
+            for u, (t0, t1) in enumerate(tb_groups):
+                for t in range(t0, t1):
+                    nc.scalar.activation(
+                        tg[a][:, t, :],
+                        tbt[u][:, t - t0, :].indirect(idx2[:, a * LIST_COLS : (a + 1) * LIST_COLS]),
+                        COPY,
+                    )
+
+        def gather_tz(a):
+            for h in range(HALVES):
+                nc.scalar.activation(
+                    zg[a][:, h, :],
+                    tzt[:, h, :].indirect(idx3[:, a * LIST_COLS : (a + 1) * LIST_COLS]),
+                    COPY,
+                )
+
+        for z in range(PASSES):
+            nc.scalar.copy(
+                out=wp[:, z, :].bitcast(U16).rearrange("p (t m) -> p t m", t=PACK),
+                in_=w_raw[:, z, :].bitcast(U16).rearrange("p (m t) -> p t m", t=PACK),
+            )
+        for a in range(CHUNKS):
+            gather_tb(a)
+        for a in range(CHUNKS):
+            gather_tz(a)
+
+        rw_all = ps.tile([P, J], F32, name="rw_all")
+        for a in range(CHUNKS):
+            nc.tensor.transpose(
+                rw_all[:, a * CHUNK : (a + 1) * CHUNK], rwc[:, a : a + 1].to_broadcast([P, P]), ident[:]
+            )
+
+        acc = [ps.tile([P, PACK, CHUNK], F32, name=f"acc{a}") for a in range(CHUNKS)]
+        for a in range(CHUNKS):
+            cols = slice(a * CHUNK, (a + 1) * CHUNK)
+            for z in range(PASSES):
+                for t in range(PACK):
+                    nc.tensor.matmul_mx(
+                        out=acc[a][:, t, :],
+                        lhsT=wp[:, z, 2 * P * t : 2 * P * (t + 1)].bitcast(E2M1X4),
+                        lhsT_scale=wsp[:, z, P * t : P * (t + 1)],
+                        rhs=gw[z][:, cols].bitcast(E4M3X4),
+                        rhs_scale=gs[z][:, cols],
+                        start=(z == 0 and t == 0),
+                        stop=(z == PASSES - 1 and t == PACK - 1),
+                    )
+
+        hb = [sb.tile([P, CHUNK * PACK], BF16, name=f"hb{a}", align_bytes=64) for a in range(CHUNKS)]
+        hq = [sb.tile([P, CHUNK], U32, name=f"hq{a}", align_bytes=64) for a in range(CHUNKS)]
+        hs = [sb.tile([P, CHUNK], U8, name=f"hs{a}", align_bytes=64) for a in range(CHUNKS)]
+        acc2 = [ps.tile([P, HALVES, CHUNK], F32, name=f"acc2{a}") for a in range(CHUNKS)]
+        fl = [sb.tile([P, HALVES, CHUNK], F32, name=f"fl{a}", align_bytes=64) for a in range(CHUNKS)]
+        res = [sb.tile([P, HALVES, CHUNK], F32, name=f"res{a}", align_bytes=64) for a in range(CHUNKS)]
+        wbs_bytes = wbs[:].bitcast(U8)
+        out_rows = out.rearrange("(h p) j -> p h j", p=P)
+
+        def hidden(a):
+            nc.vector.tensor_tensor(
+                hb[a][:].rearrange("p (c i t) -> p c t i", i=2, t=PACK),
+                acc[a][:].rearrange("p t (c i) -> p c t i", i=2),
+                tg[a][:].rearrange("p t (c i) -> p c t i", i=2),
+                MAX,
+            )
+
+        def second(a):
+            nc.vector.quantize_mx(out=hq[a][:].bitcast(E4M3X4), scales=hs[a][:], in_=hb[a][:])
+            for h in range(HALVES):
+                nc.tensor.matmul_mx(
+                    out=acc2[a][:, h, :],
+                    lhsT=wbw[:, P * h : P * (h + 1)].bitcast(E5M2X4),
+                    lhsT_scale=wbs_bytes[:, 0, P * h : P * (h + 1)],
+                    rhs=hq[a][:].bitcast(E4M3X4),
+                    rhs_scale=hs[a][:],
+                    start=True,
+                    stop=True,
+                )
+
+        def floor(a):
+            nc.vector.tensor_tensor(fl[a][:], acc2[a][:], zg[a][:], MAX)
+
+        def weigh(a):
+            cols = slice(a * CHUNK, (a + 1) * CHUNK)
+            nc.vector.tensor_tensor(
+                res[a][:], fl[a][:], rw_all[:, cols].unsqueeze(1).to_broadcast([P, HALVES, CHUNK]), MULT
+            )
+            nc.sync.dma_start(out=out_rows[:, :, cols], in_=res[a][:])
+
+        stages = [hidden, second, floor, weigh]
+        for step in range(CHUNKS + len(stages) - 1):
+            for s in range(len(stages)):
+                a = step - s
+                if 0 <= a < CHUNKS:
+                    stages[s](a)

@@ -28,9 +28,9 @@ HALVES = N // P
 LIST_COLS = CHUNK // 16
 
 
-def load_scale_rows(queue, plane, scales):
+def load_scale_rows(queue, plane, scales, quadrants=range(4)):
     words = scales.bitcast(I32)
-    for q in range(4):
+    for q in quadrants:
         queue.dma_start(
             out=plane[32 * q : 32 * q + 4, :, :],
             in_=words[:, 4 * q : 4 * q + 4, :].rearrange("z r c -> r z c"),
@@ -53,66 +53,58 @@ def tile_list_picked_abovetable_floored_kernel(
         wbs = sb.tile([P, 1, N // 4], I32, name="wbs", align_bytes=64)
         xw = [sb.tile([P, T], I32, name=f"xw{z}", align_bytes=64) for z in range(PASSES)]
         w_raw = sb.tile([P, PASSES, R // 2], I32, name="w_raw", align_bytes=64)
-        tb_groups = [(0, 2), (2, 3), (3, 4)]
-        tbt = [sb.tile([P, t1 - t0, V], F32, name=f"tbt{t0}", align_bytes=64) for t0, t1 in tb_groups]
+        tbt = [sb.tile([P, 2, V], F32, name=f"tbt{u}", align_bytes=64) for u in range(2)]
         tzt = sb.tile([P, HALVES, Z], F32, name="tzt", align_bytes=64)
         wbw = sb.tile([P, N], I32, name="wbw", align_bytes=64)
         rwc = sb.tile([P, CHUNKS], F32, name="rwc", align_bytes=64)
         ident = sb.tile([P, P], F32, name="ident", align_bytes=64)
 
         nc.vector.memset(xs[:], 0)
-        nc.vector.memset(ws_raw[:], 0)
-        nc.gpsimd.memset(wbs[:], 0)
+        nc.gpsimd.memset(ws_raw[:], 0)
 
         tb_rows = tb.rearrange("(p t) v -> p t v", t=PACK)
         nc.sync.dma_start(idx[:], offs)
         nc.sync.dma_start(out=w_raw[:], in_=w_words.bitcast(I32).rearrange("z p c -> p z c"))
         load_scale_rows(nc.sync, xs, xt_scales)
-        nc.sync.dma_start(idx2[:], offs2)
-        nc.sync.dma_start(out=tbt[0][:], in_=tb_rows[:, 0:2, :])
         nc.sync.dma_start(out=xw[0][:], in_=xt_words[0].rearrange("p c r -> p (c r)").bitcast(I32))
+        nc.sync.dma_start(out=tbt[0][:], in_=tb_rows[:, 0:2, :])
         load_scale_rows(nc.sync, ws_raw, w_scales)
-        nc.sync.dma_start(out=tbt[1][:], in_=tb_rows[:, 2:3, :])
+        nc.sync.dma_start(idx2[:], offs2)
         nc.sync.dma_start(out=xw[1][:], in_=xt_words[1].rearrange("p c r -> p (c r)").bitcast(I32))
-        nc.sync.dma_start(out=tbt[2][:], in_=tb_rows[:, 3:4, :])
+        nc.sync.dma_start(out=tbt[1][:], in_=tb_rows[:, 2:4, :])
         nc.sync.dma_start(out=tzt[:], in_=tz.rearrange("(h p) z -> p h z", p=P))
         nc.sync.dma_start(idx3[:], offs3)
         nc.sync.dma_start(out=wbw[:], in_=wb_words[0].rearrange("p c r -> p (c r)").bitcast(I32))
+        nc.gpsimd.memset(wbs[:], 0)
         load_scale_rows(nc.sync, wbs, wb_scales)
         make_identity(nc, ident[:])
-        with nc.allow_non_contiguous_dma(reason="one weight to a partition"):
-            nc.gpsimd.dma_start(out=rwc[:], in_=rw.rearrange("o (c p) -> p (o c)", p=P))
+        nc.gpsimd.dma_start(out=rwc[:], in_=rw.rearrange("o (p c) -> p (o c)", p=P))
 
         xs_bytes = xs[:].bitcast(U8)
         gs = [sb.tile([P, J], U8, name=f"gs{z}", align_bytes=64) for z in range(PASSES)]
         gw = [sb.tile([P, J], U32, name=f"gw{z}", align_bytes=64) for z in range(PASSES)]
         wp = sb.tile([P, PASSES, 2 * R], U8, name="wp", align_bytes=64)
         wsp = sb.tile([P, PASSES, R], U8, name="wsp", align_bytes=64)
-        for z in range(PASSES):
-            nc.vector.tensor_copy(gs[z][:], xs_bytes[:, z, :].indirect(idx[:]))
-        for z in range(PASSES):
+
+        def deal_w_scales(z):
             nc.vector.tensor_copy(
                 out=wsp[:, z, :].rearrange("p (t m) -> p t m", t=PACK),
                 in_=ws_raw[:, z, :].bitcast(U8).rearrange("p (m t) -> p t m", t=PACK),
             )
+
+        nc.vector.tensor_copy(gs[0][:], xs_bytes[:, 0, :].indirect(idx[:]))
+        nc.vector.tensor_copy(gw[0][:], xw[0][:].bitcast(U32).indirect(idx[:]))
+        deal_w_scales(0)
+        nc.vector.tensor_copy(gs[1][:], xs_bytes[:, 1, :].indirect(idx[:]))
+        deal_w_scales(1)
         for a in range(CHUNKS):
-            for z in range(PASSES):
-                nc.vector.tensor_copy(
-                    gw[z][:, a * CHUNK : (a + 1) * CHUNK],
-                    xw[z][:].bitcast(U32).indirect(idx[:, a * LIST_COLS : (a + 1) * LIST_COLS]),
-                )
+            nc.vector.tensor_copy(
+                gw[1][:, a * CHUNK : (a + 1) * CHUNK],
+                xw[1][:].bitcast(U32).indirect(idx[:, a * LIST_COLS : (a + 1) * LIST_COLS]),
+            )
 
-        tg = [sb.tile([P, PACK, CHUNK], F32, name=f"tg{a}", align_bytes=64) for a in range(CHUNKS)]
+        tg = sb.tile([P, PACK, J], F32, name="tg", align_bytes=64)
         zg = [sb.tile([P, HALVES, CHUNK], F32, name=f"zg{a}", align_bytes=64) for a in range(CHUNKS)]
-
-        def gather_tb(a):
-            for u, (t0, t1) in enumerate(tb_groups):
-                for t in range(t0, t1):
-                    nc.scalar.activation(
-                        tg[a][:, t, :],
-                        tbt[u][:, t - t0, :].indirect(idx2[:, a * LIST_COLS : (a + 1) * LIST_COLS]),
-                        COPY,
-                    )
 
         def gather_tz(a):
             for h in range(HALVES):
@@ -127,15 +119,27 @@ def tile_list_picked_abovetable_floored_kernel(
                 out=wp[:, z, :].bitcast(U16).rearrange("p (t m) -> p t m", t=PACK),
                 in_=w_raw[:, z, :].bitcast(U16).rearrange("p (m t) -> p t m", t=PACK),
             )
-        for a in range(CHUNKS):
-            gather_tb(a)
+
+        def listed_tb(t, c0, c1):
+            return tbt[t // 2][:, t % 2, :].indirect(idx2[:, c0 // 16 : c1 // 16])
+
+        nc.scalar.activation(tg[:, 0, :], tbt[0][:].rearrange("p e v -> p (e v)").indirect(idx2[:]), COPY)
+        nc.scalar.activation(tg[:, 1, 0:CHUNK], listed_tb(1, 0, CHUNK), COPY)
+        nc.scalar.activation(tg[:, 2, 0:CHUNK], listed_tb(2, 0, CHUNK), COPY)
+        nc.vector.tensor_copy(tg[:, 3, 0:CHUNK], listed_tb(3, 0, CHUNK))
+        nc.scalar.activation(tg[:, 1, CHUNK:J], listed_tb(1, CHUNK, J), COPY)
+        nc.scalar.activation(tg[:, 2, CHUNK:J], listed_tb(2, CHUNK, J), COPY)
+        for a in range(1, CHUNKS):
+            nc.scalar.activation(
+                tg[:, 3, a * CHUNK : (a + 1) * CHUNK], listed_tb(3, a * CHUNK, (a + 1) * CHUNK), COPY
+            )
         for a in range(CHUNKS):
             gather_tz(a)
 
         rw_all = ps.tile([P, J], F32, name="rw_all")
         for a in range(CHUNKS):
             nc.tensor.transpose(
-                rw_all[:, a * CHUNK : (a + 1) * CHUNK], rwc[:, a : a + 1].to_broadcast([P, P]), ident[:]
+                rw_all[:, a :: CHUNKS], rwc[:, a : a + 1].to_broadcast([P, P]), ident[:]
             )
 
         acc = [ps.tile([P, PACK, CHUNK], F32, name=f"acc{a}") for a in range(CHUNKS)]
@@ -166,7 +170,7 @@ def tile_list_picked_abovetable_floored_kernel(
             nc.vector.tensor_tensor(
                 hb[a][:].rearrange("p (c i t) -> p c t i", i=2, t=PACK),
                 acc[a][:].rearrange("p t (c i) -> p c t i", i=2),
-                tg[a][:].rearrange("p t (c i) -> p c t i", i=2),
+                tg[:, :, a * CHUNK : (a + 1) * CHUNK].rearrange("p t (c i) -> p c t i", i=2),
                 MAX,
             )
 

@@ -53,32 +53,42 @@ def tile_list_picked_abovetable_floored_kernel(
         wbs = sb.tile([P, 1, N // 4], I32, name="wbs", align_bytes=64)
         xw = [sb.tile([P, T], I32, name=f"xw{z}", align_bytes=64) for z in range(PASSES)]
         w_raw = sb.tile([P, PASSES, R // 2], I32, name="w_raw", align_bytes=64)
-        tbt = [sb.tile([P, 2, V], F32, name=f"tbt{u}", align_bytes=64) for u in range(2)]
+        tb_groups = [(0, 2), (2, 4)]
+        tbt = [sb.tile([P, t1 - t0, V], F32, name=f"tbt{t0}", align_bytes=64) for t0, t1 in tb_groups]
+        tb_plane = [tbt[u][:, t - t0, :] for u, (t0, t1) in enumerate(tb_groups) for t in range(t0, t1)]
         tzt = sb.tile([P, HALVES, Z], F32, name="tzt", align_bytes=64)
         wbw = sb.tile([P, N], I32, name="wbw", align_bytes=64)
         rwc = sb.tile([P, CHUNKS], F32, name="rwc", align_bytes=64)
         ident = sb.tile([P, P], F32, name="ident", align_bytes=64)
 
         nc.vector.memset(xs[:], 0)
-        nc.gpsimd.memset(ws_raw[:], 0)
+        nc.vector.memset(ws_raw[:], 0)
 
         tb_rows = tb.rearrange("(p t) v -> p t v", t=PACK)
+
+        def load_tb(u):
+            nc.sync.dma_start(out=tbt[u][:], in_=tb_rows[:, tb_groups[u][0] : tb_groups[u][1], :])
+
         nc.sync.dma_start(idx[:], offs)
         nc.sync.dma_start(out=w_raw[:], in_=w_words.bitcast(I32).rearrange("z p c -> p z c"))
         load_scale_rows(nc.sync, xs, xt_scales)
         nc.sync.dma_start(out=xw[0][:], in_=xt_words[0].rearrange("p c r -> p (c r)").bitcast(I32))
-        nc.sync.dma_start(out=tbt[0][:], in_=tb_rows[:, 0:2, :])
-        load_scale_rows(nc.sync, ws_raw, w_scales)
+        load_tb(0)
         nc.sync.dma_start(idx2[:], offs2)
+        load_scale_rows(nc.sync, ws_raw, w_scales)
         nc.sync.dma_start(out=xw[1][:], in_=xt_words[1].rearrange("p c r -> p (c r)").bitcast(I32))
-        nc.sync.dma_start(out=tbt[1][:], in_=tb_rows[:, 2:4, :])
+        load_tb(1)
         nc.sync.dma_start(out=tzt[:], in_=tz.rearrange("(h p) z -> p h z", p=P))
-        nc.sync.dma_start(idx3[:], offs3)
         nc.sync.dma_start(out=wbw[:], in_=wb_words[0].rearrange("p c r -> p (c r)").bitcast(I32))
+        nc.sync.dma_start(idx3[:], offs3)
+        nc.gpsimd.dma_start(out=rwc[:], in_=rw.rearrange("o (p c) -> p (o c)", p=P))
+        make_identity(nc, ident[:])
         nc.gpsimd.memset(wbs[:], 0)
         load_scale_rows(nc.sync, wbs, wb_scales)
-        make_identity(nc, ident[:])
-        nc.gpsimd.dma_start(out=rwc[:], in_=rw.rearrange("o (p c) -> p (o c)", p=P))
+
+        rw_all = ps.tile([P, J], F32, name="rw_all")
+        for c in range(CHUNKS):
+            nc.tensor.transpose(rw_all[:, c::CHUNKS], rwc[:, c : c + 1].to_broadcast([P, P]), ident[:])
 
         xs_bytes = xs[:].bitcast(U8)
         gs = [sb.tile([P, J], U8, name=f"gs{z}", align_bytes=64) for z in range(PASSES)]
@@ -95,15 +105,15 @@ def tile_list_picked_abovetable_floored_kernel(
         nc.vector.tensor_copy(gs[0][:], xs_bytes[:, 0, :].indirect(idx[:]))
         nc.vector.tensor_copy(gw[0][:], xw[0][:].bitcast(U32).indirect(idx[:]))
         deal_w_scales(0)
-        nc.vector.tensor_copy(gs[1][:], xs_bytes[:, 1, :].indirect(idx[:]))
         deal_w_scales(1)
+        nc.vector.tensor_copy(gs[1][:], xs_bytes[:, 1, :].indirect(idx[:]))
         for a in range(CHUNKS):
             nc.vector.tensor_copy(
                 gw[1][:, a * CHUNK : (a + 1) * CHUNK],
                 xw[1][:].bitcast(U32).indirect(idx[:, a * LIST_COLS : (a + 1) * LIST_COLS]),
             )
 
-        tg = sb.tile([P, PACK, J], F32, name="tg", align_bytes=64)
+        tg = [sb.tile([P, PACK, CHUNK], F32, name=f"tg{a}", align_bytes=64) for a in range(CHUNKS)]
         zg = [sb.tile([P, HALVES, CHUNK], F32, name=f"zg{a}", align_bytes=64) for a in range(CHUNKS)]
 
         def gather_tz(a):
@@ -120,29 +130,25 @@ def tile_list_picked_abovetable_floored_kernel(
                 in_=w_raw[:, z, :].bitcast(U16).rearrange("p (m t) -> p t m", t=PACK),
             )
 
-        def listed_tb(t, c0, c1):
-            return tbt[t // 2][:, t % 2, :].indirect(idx2[:, c0 // 16 : c1 // 16])
-
-        nc.scalar.activation(tg[:, 0, :], tbt[0][:].rearrange("p e v -> p (e v)").indirect(idx2[:]), COPY)
-        nc.scalar.activation(tg[:, 1, 0:CHUNK], listed_tb(1, 0, CHUNK), COPY)
-        nc.scalar.activation(tg[:, 2, 0:CHUNK], listed_tb(2, 0, CHUNK), COPY)
-        nc.vector.tensor_copy(tg[:, 3, 0:CHUNK], listed_tb(3, 0, CHUNK))
-        nc.scalar.activation(tg[:, 1, CHUNK:J], listed_tb(1, CHUNK, J), COPY)
-        nc.scalar.activation(tg[:, 2, CHUNK:J], listed_tb(2, CHUNK, J), COPY)
-        for a in range(1, CHUNKS):
-            nc.scalar.activation(
-                tg[:, 3, a * CHUNK : (a + 1) * CHUNK], listed_tb(3, a * CHUNK, (a + 1) * CHUNK), COPY
-            )
+        rw_sb = sb.tile([P, CHUNKS - 1, HALVES, CHUNK], F32, name="rw_sb", align_bytes=64)
+        nc.scalar.copy(
+            out=rw_sb[:],
+            in_=rw_all[:, 0 : J - CHUNK]
+            .rearrange("p (a j) -> p a j", j=CHUNK)
+            .unsqueeze(2)
+            .to_broadcast([P, CHUNKS - 1, HALVES, CHUNK]),
+        )
+        for a in range(CHUNKS):
+            for t in range(PACK):
+                listed = tb_plane[t].indirect(idx2[:, a * LIST_COLS : (a + 1) * LIST_COLS])
+                if (a, t) == (0, PACK - 1):
+                    nc.vector.tensor_copy(tg[a][:, t, :], listed)
+                else:
+                    nc.scalar.activation(tg[a][:, t, :], listed, COPY)
         for a in range(CHUNKS):
             gather_tz(a)
 
-        rw_all = ps.tile([P, J], F32, name="rw_all")
-        for a in range(CHUNKS):
-            nc.tensor.transpose(
-                rw_all[:, a :: CHUNKS], rwc[:, a : a + 1].to_broadcast([P, P]), ident[:]
-            )
-
-        acc = [ps.tile([P, PACK, CHUNK], F32, name=f"acc{a}") for a in range(CHUNKS)]
+        acc = [ps.tile([P, PACK, CHUNK], F32, name=f"acc{a}", tag=f"bank{a}") for a in range(CHUNKS)]
         for a in range(CHUNKS):
             cols = slice(a * CHUNK, (a + 1) * CHUNK)
             for z in range(PASSES):
@@ -170,7 +176,7 @@ def tile_list_picked_abovetable_floored_kernel(
             nc.vector.tensor_tensor(
                 hb[a][:].rearrange("p (c i t) -> p c t i", i=2, t=PACK),
                 acc[a][:].rearrange("p t (c i) -> p c t i", i=2),
-                tg[:, :, a * CHUNK : (a + 1) * CHUNK].rearrange("p t (c i) -> p c t i", i=2),
+                tg[a][:].rearrange("p t (c i) -> p c t i", i=2),
                 MAX,
             )
 
@@ -187,19 +193,23 @@ def tile_list_picked_abovetable_floored_kernel(
                     stop=True,
                 )
 
-        def floor(a):
+        def finish_early(a):
             nc.vector.tensor_tensor(fl[a][:], acc2[a][:], zg[a][:], MAX)
+            nc.gpsimd.tensor_tensor(res[a][:], fl[a][:], rw_sb[:, a, :, :], MULT)
+            nc.sync.dma_start(out=out_rows[:, :, a * CHUNK : (a + 1) * CHUNK], in_=res[a][:])
 
-        def weigh(a):
-            cols = slice(a * CHUNK, (a + 1) * CHUNK)
-            nc.vector.tensor_tensor(
-                res[a][:], fl[a][:], rw_all[:, cols].unsqueeze(1).to_broadcast([P, HALVES, CHUNK]), MULT
-            )
-            nc.sync.dma_start(out=out_rows[:, :, cols], in_=res[a][:])
-
-        stages = [hidden, second, floor, weigh]
-        for step in range(CHUNKS + len(stages) - 1):
-            for s in range(len(stages)):
-                a = step - s
-                if 0 <= a < CHUNKS:
-                    stages[s](a)
+        hidden(0)
+        hidden(1)
+        second(0)
+        hidden(2)
+        second(1)
+        finish_early(0)
+        second(2)
+        finish_early(1)
+        last = CHUNKS - 1
+        cols = slice(last * CHUNK, J)
+        for h in range(HALVES):
+            nc.vector.tensor_tensor(fl[last][:, h, :], acc2[last][:, h, :], zg[last][:, h, :], MAX)
+        for h in range(HALVES):
+            nc.vector.tensor_tensor(res[last][:, h, :], fl[last][:, h, :], rw_all[:, cols], MULT)
+            nc.scalar.dma_start(out=out_rows[:, h, cols], in_=res[last][:, h, :])

@@ -97,7 +97,7 @@ def tile_list_picked_abovetable_floored_kernel(
         wsp = sb.tile([P, PASSES, R], U8, name="wsp", align_bytes=64)
 
         def deal_w_scales(z):
-            nc.vector.tensor_copy(
+            nc.gpsimd.tensor_copy(
                 out=wsp[:, z, :].rearrange("p (t m) -> p t m", t=PACK),
                 in_=ws_raw[:, z, :].bitcast(U8).rearrange("p (m t) -> p t m", t=PACK),
             )

from contextlib import ExitStack

import concourse.mybir as mybir
from concourse.masks import make_identity

K, T, J, R, V, N, Z = 1024, 1024, 384, 512, 512, 256, 512
FLOPS = 2 * K * R * J + 2 * R * N * J

F32 = mybir.dt.float32
BF16 = mybir.dt.bfloat16
I32 = mybir.dt.int32
U32 = mybir.dt.uint32
U16 = mybir.dt.uint16
U8 = mybir.dt.uint8
E4M3X4 = mybir.dt.float8_e4m3fn_x4
E5M2X4 = mybir.dt.float8_e5m2_x4
E2M1X4 = mybir.dt.float4_e2m1fn_x4
MAX = mybir.AluOpType.max
MULT = mybir.AluOpType.mult
COPY = mybir.ActivationFunctionType.Copy

P = 128
PACK = 4
PASSES = K // (P * PACK)
CHUNK = 128
CHUNKS = J // CHUNK
HALVES = N // P
LIST_COLS = CHUNK // 16


def load_scale_rows(queue, plane, scales, quadrants=range(4)):
    words = scales.bitcast(I32)
    for q in quadrants:
        queue.dma_start(
            out=plane[32 * q : 32 * q + 4, :, :],
            in_=words[:, 4 * q : 4 * q + 4, :].rearrange("z r c -> r z c"),
        )


def tile_list_picked_abovetable_floored_kernel(
    tc, xt_words, xt_scales, w_words, w_scales, tb, wb_words, wb_scales, tz, rw, offs, offs2, offs3, out
):
    nc = tc.nc
    with ExitStack() as ctx:
        sb = ctx.enter_context(tc.tile_pool(name="sb", bufs=1))
        ps = ctx.enter_context(tc.psum_pool(name="ps", bufs=1))

        idx = sb.tile([P, J // 16], U16, name="idx")
        idx2 = sb.tile([P, J // 16], U16, name="idx2")
        idx3 = sb.tile([P, J // 16], U16, name="idx3")
        xs = sb.tile([P, PASSES, T // 4], I32, name="xs", align_bytes=64)
        ws_raw = sb.tile([P, PASSES, R // 4], I32, name="ws_raw", align_bytes=64)
        wbs = sb.tile([P, 1, N // 4], I32, name="wbs", align_bytes=64)
        xw = [sb.tile([P, T], I32, name=f"xw{z}", align_bytes=64) for z in range(PASSES)]
        w_raw = sb.tile([P, PASSES, R // 2], I32, name="w_raw", align_bytes=64)
        tb_groups = [(0, 2), (2, 4)]
        tbt = [sb.tile([P, t1 - t0, V], F32, name=f"tbt{t0}", align_bytes=64) for t0, t1 in tb_groups]
        tb_plane = [tbt[u][:, t - t0, :] for u, (t0, t1) in enumerate(tb_groups) for t in range(t0, t1)]
        tzt = sb.tile([P, HALVES, Z], F32, name="tzt", align_bytes=64)
        wbw = sb.tile([P, N], I32, name="wbw", align_bytes=64)
        rwc = sb.tile([P, CHUNKS], F32, name="rwc", align_bytes=64)
        ident = sb.tile([P, P], F32, name="ident", align_bytes=64)

        nc.vector.memset(xs[:], 0)
        nc.vector.memset(ws_raw[:], 0)

        tb_rows = tb.rearrange("(p t) v -> p t v", t=PACK)

        def load_tb(u):
            nc.sync.dma_start(out=tbt[u][:], in_=tb_rows[:, tb_groups[u][0] : tb_groups[u][1], :])

        nc.sync.dma_start(idx[:], offs)
        nc.sync.dma_start(out=w_raw[:], in_=w_words.bitcast(I32).rearrange("z p c -> p z c"))
        load_scale_rows(nc.sync, xs, xt_scales)
        nc.sync.dma_start(out=xw[0][:], in_=xt_words[0].rearrange("p c r -> p (c r)").bitcast(I32))
        load_tb(0)
        nc.sync.dma_start(idx2[:], offs2)
        load_scale_rows(nc.sync, ws_raw, w_scales)
        nc.sync.dma_start(out=xw[1][:], in_=xt_words[1].rearrange("p c r -> p (c r)").bitcast(I32))
        load_tb(1)
        nc.sync.dma_start(out=tzt[:], in_=tz.rearrange("(h p) z -> p h z", p=P))
        nc.sync.dma_start(out=wbw[:], in_=wb_words[0].rearrange("p c r -> p (c r)").bitcast(I32))
        nc.sync.dma_start(idx3[:], offs3)
        nc.gpsimd.dma_start(out=rwc[:], in_=rw.rearrange("o (p c) -> p (o c)", p=P))
        make_identity(nc, ident[:])
        nc.gpsimd.memset(wbs[:], 0)
        load_scale_rows(nc.sync, wbs, wb_scales)

        rw_all = ps.tile([P, J], F32, name="rw_all")
        for c in range(CHUNKS):
            nc.tensor.transpose(rw_all[:, c::CHUNKS], rwc[:, c : c + 1].to_broadcast([P, P]), ident[:])

        xs_bytes = xs[:].bitcast(U8)
        gs = [sb.tile([P, J], U8, name=f"gs{z}", align_bytes=64) for z in range(PASSES)]
        gw = [sb.tile([P, J], U32, name=f"gw{z}", align_bytes=64) for z in range(PASSES)]
        wp = sb.tile([P, PASSES, 2 * R], U8, name="wp", align_bytes=64)
        wsp = sb.tile([P, PASSES, R], U8, name="wsp", align_bytes=64)

        def deal_w_scales(z):
            nc.gpsimd.tensor_copy(
                out=wsp[:, z, :].rearrange("p (t m) -> p t m", t=PACK),
                in_=ws_raw[:, z, :].bitcast(U8).rearrange("p (m t) -> p t m", t=PACK),
            )

        nc.vector.tensor_copy(gs[0][:], xs_bytes[:, 0, :].indirect(idx[:]))
        nc.vector.tensor_copy(gw[0][:], xw[0][:].bitcast(U32).indirect(idx[:]))
        deal_w_scales(0)
        deal_w_scales(1)
        nc.vector.tensor_copy(gs[1][:], xs_bytes[:, 1, :].indirect(idx[:]))
        for a in range(CHUNKS):
            nc.vector.tensor_copy(
                gw[1][:, a * CHUNK : (a + 1) * CHUNK],
                xw[1][:].bitcast(U32).indirect(idx[:, a * LIST_COLS : (a + 1) * LIST_COLS]),
            )

        tg = [sb.tile([P, PACK, CHUNK], F32, name=f"tg{a}", align_bytes=64) for a in range(CHUNKS)]
        zg = [sb.tile([P, HALVES, CHUNK], F32, name=f"zg{a}", align_bytes=64) for a in range(CHUNKS)]

        def gather_tz(a):
            for h in range(HALVES):
                nc.scalar.activation(
                    zg[a][:, h, :],
                    tzt[:, h, :].indirect(idx3[:, a * LIST_COLS : (a + 1) * LIST_COLS]),
                    COPY,
                )

        for z in range(PASSES):
            nc.scalar.copy(
                out=wp[:, z, :].bitcast(U16).rearrange("p (t m) -> p t m", t=PACK),
                in_=w_raw[:, z, :].bitcast(U16).rearrange("p (m t) -> p t m", t=PACK),
            )

        rw_sb = sb.tile([P, CHUNKS - 1, HALVES, CHUNK], F32, name="rw_sb", align_bytes=64)
        nc.scalar.copy(
            out=rw_sb[:],
            in_=rw_all[:, 0 : J - CHUNK]
            .rearrange("p (a j) -> p a j", j=CHUNK)
            .unsqueeze(2)
            .to_broadcast([P, CHUNKS - 1, HALVES, CHUNK]),
        )
        for a in range(CHUNKS):
            for t in range(PACK):
                listed = tb_plane[t].indirect(idx2[:, a * LIST_COLS : (a + 1) * LIST_COLS])
                if (a, t) == (0, PACK - 1):
                    nc.vector.tensor_copy(tg[a][:, t, :], listed)
                else:
                    nc.scalar.activation(tg[a][:, t, :], listed, COPY)
        for a in range(CHUNKS):
            gather_tz(a)

        acc = [ps.tile([P, PACK, CHUNK], F32, name=f"acc{a}", tag=f"bank{a}") for a in range(CHUNKS)]
        for a in range(CHUNKS):
            cols = slice(a * CHUNK, (a + 1) * CHUNK)
            for z in range(PASSES):
                for t in range(PACK):
                    nc.tensor.matmul_mx(
                        out=acc[a][:, t, :],
                        lhsT=wp[:, z, 2 * P * t : 2 * P * (t + 1)].bitcast(E2M1X4),
                        lhsT_scale=wsp[:, z, P * t : P * (t + 1)],
                        rhs=gw[z][:, cols].bitcast(E4M3X4),
                        rhs_scale=gs[z][:, cols],
                        start=(z == 0 and t == 0),
                        stop=(z == PASSES - 1 and t == PACK - 1),
                    )

        hb = [sb.tile([P, CHUNK * PACK], BF16, name=f"hb{a}", align_bytes=64) for a in range(CHUNKS)]
        hq = [sb.tile([P, CHUNK], U32, name=f"hq{a}", align_bytes=64) for a in range(CHUNKS)]
        hs = [sb.tile([P, CHUNK], U8, name=f"hs{a}", align_bytes=64) for a in range(CHUNKS)]
        acc2 = [ps.tile([P, HALVES, CHUNK], F32, name=f"acc2{a}") for a in range(CHUNKS)]
        fl = [sb.tile([P, HALVES, CHUNK], F32, name=f"fl{a}", align_bytes=64) for a in range(CHUNKS)]
        res = [sb.tile([P, HALVES, CHUNK], F32, name=f"res{a}", align_bytes=64) for a in range(CHUNKS)]
        wbs_bytes = wbs[:].bitcast(U8)
        out_rows = out.rearrange("(h p) j -> p h j", p=P)

        def hidden(a):
            nc.vector.tensor_tensor(
                hb[a][:].rearrange("p (c i t) -> p c t i", i=2, t=PACK),
                acc[a][:].rearrange("p t (c i) -> p c t i", i=2),
                tg[a][:].rearrange("p t (c i) -> p c t i", i=2),
                MAX,
            )

        def second(a):
            nc.vector.quantize_mx(out=hq[a][:].bitcast(E4M3X4), scales=hs[a][:], in_=hb[a][:])
            for h in range(HALVES):
                nc.tensor.matmul_mx(
                    out=acc2[a][:, h, :],
                    lhsT=wbw[:, P * h : P * (h + 1)].bitcast(E5M2X4),
                    lhsT_scale=wbs_bytes[:, 0, P * h : P * (h + 1)],
                    rhs=hq[a][:].bitcast(E4M3X4),
                    rhs_scale=hs[a][:],
                    start=True,
                    stop=True,
                )

        def finish_early(a):
            nc.vector.tensor_tensor(fl[a][:], acc2[a][:], zg[a][:], MAX)
            nc.gpsimd.tensor_tensor(res[a][:], fl[a][:], rw_sb[:, a, :, :], MULT)
            nc.sync.dma_start(out=out_rows[:, :, a * CHUNK : (a + 1) * CHUNK], in_=res[a][:])

        hidden(0)
        hidden(1)
        second(0)
        hidden(2)
        second(1)
        finish_early(0)
        second(2)
        finish_early(1)
        last = CHUNKS - 1
        cols = slice(last * CHUNK, J)
        for h in range(HALVES):
            nc.vector.tensor_tensor(fl[last][:, h, :], acc2[last][:, h, :], zg[last][:, h, :], MAX)
        for h in range(HALVES):
            nc.vector.tensor_tensor(res[last][:, h, :], fl[last][:, h, :], rw_all[:, cols], MULT)
            nc.scalar.dma_start(out=out_rows[:, h, cols], in_=res[last][:, h, :])
